import numpy as np
import ml_dtypes


def mxq(x, axis, fmt="e4m3"):
    dtype, down = {"e4m3": (ml_dtypes.float8_e4m3fn, 7), "e5m2": (ml_dtypes.float8_e5m2, 14)}[fmt]
    v = np.moveaxis(np.asarray(x, np.float32).astype(ml_dtypes.bfloat16).astype(np.float64), axis, -1)
    blocks = v.reshape(v.shape[:-1] + (-1, 32))
    amax = np.abs(blocks).max(-1, keepdims=True)
    byte = np.maximum(np.where(amax > 0, np.frexp(amax)[1] - 1 + 127, 0) - down, 1)
    scale = np.exp2(byte - 127.0)
    codes = (blocks / scale).astype(np.float32).astype(dtype).astype(np.float64)
    return np.moveaxis((codes * scale).reshape(v.shape), -1, axis)


WIDE = False


def mx_kscale(k):
    if not WIDE:
        return np.ones(k)
    levels = np.array([10, -10, 5, -5, 0])
    if k % 512:
        return np.exp2(np.random.permutation(np.resize(levels, k // 32))).repeat(32)
    a = np.empty((k // 512, 16))
    for p in range(k // 512):
        a[p, :8] = np.random.permutation(np.resize(levels, 8))
        for g in range(8):
            far = levels[np.abs(levels - a[p, g]) >= 10]
            a[p, g + 8] = far[np.random.randint(len(far))]
    return np.exp2(a.ravel()).repeat(32)


def f64(x):
    return np.asarray(x).astype(np.float64)


def striped(idx):
    return np.tile(idx.reshape(-1, 16).T, (8, 1)).astype(np.uint16)


def unstriped(offs):
    return offs[:16].T.reshape(-1).astype(np.int64)


E2M1 = np.array([0.0, 0.5, 1.0, 1.5, 2.0, 3.0, 4.0, 6.0, -0.0, -0.5, -1.0, -1.5, -2.0, -3.0, -4.0, -6.0])


def pack_weight(w, fmt):
    k, n = w.shape
    w = f64(np.asarray(w, np.float32).astype(ml_dtypes.bfloat16)).reshape(k // 32, 32, n)
    amax = np.abs(w).max(1)
    if fmt == "e4m3":
        byte = np.frexp(amax)[1] - 1 + 127 - 7
    else:
        mant, ex = np.frexp(amax / 6.0)
        byte = np.where(mant > 0.5, ex, ex - 1) + 127
    byte = np.clip(np.where(amax > 0, byte, 1), 1, 254)
    scaled = (w * np.exp2(127.0 - byte)[:, None, :]).reshape(k, n).astype(np.float32)
    by_word = np.ascontiguousarray(scaled.reshape(k // 512, 128, 4, n).transpose(0, 1, 3, 2))
    if fmt == "e4m3":
        words = by_word.astype(ml_dtypes.float8_e4m3fn).view(np.uint8)
    else:
        c = by_word.astype(ml_dtypes.float4_e2m1fn).view(np.uint8) & 0xF
        words = (c[..., 0::2] | (c[..., 1::2] << 4)).reshape(k // 512, 128, 2 * n)
    return np.ascontiguousarray(words), np.ascontiguousarray(byte.astype(np.uint8).reshape(k // 512, 16, n))


def unpack_weight(words, scales, fmt):
    g, _, n = scales.shape
    words = np.ascontiguousarray(words).reshape(g, 128, n, -1)
    if fmt == "e4m3":
        vals = words.view(ml_dtypes.float8_e4m3fn).astype(np.float64)
    else:
        nib = np.empty((g, 128, n, 4), np.uint8)
        nib[..., 0::2] = words & 0xF
        nib[..., 1::2] = words >> 4
        vals = E2M1[nib]
    vals = vals * np.repeat(np.exp2(scales.astype(np.float64) - 127.0), 8, axis=1)[..., None]
    return vals.transpose(0, 1, 3, 2).reshape(g * 512, n)


def gelu(v):
    return 0.5 * v * (1.0 + np.tanh(np.sqrt(2.0 / np.pi) * (v + 0.044715 * v**3)))


G, K, M, T, S = 2, 1024, 128, 2048, 512


def setup_inputs():
    n = np.random.standard_normal
    s = mx_kscale(K)[:, None]
    p_w4 = pack_weight(n((K, M)) / np.sqrt(K) / s, "e2m1")
    p_w8 = pack_weight(n((K, M)) / np.sqrt(K) / s, "e4m3")
    return {
        "xT": (n((K, T)) * s).astype(np.float32),
        "c": (n((K, S)) * s).astype(np.float32),
        "w4_words": p_w4[0],
        "w4_scales": p_w4[1],
        "w8_words": p_w8[0],
        "w8_scales": p_w8[1],
        "b": (0.3 * n(128)).astype(np.float32),
        "offs": striped(np.concatenate([np.random.permutation(T)[:S] for _ in range(G)])),
    }


def reference(xT, c, w4_words, w4_scales, w8_words, w8_scales, b, offs):
    idx = unstriped(offs).reshape(G, S)
    xm_ = mxq(np.max([f64(xT)[:, idx[g]] for g in range(G)], axis=0), 0, "e4m3")
    c_ = mxq(f64(c), 0, "e4m3")
    w4_ = unpack_weight(w4_words, w4_scales, "e2m1")
    w8_ = unpack_weight(w8_words, w8_scales, "e4m3")
    y = xm_.T @ w4_ + c_.T @ w8_
    return gelu(y + f64(b)[None, :])

@@ -1,0 +1,185 @@
+from contextlib import ExitStack
+
+import concourse.mybir as mybir
+from concourse.masks import make_identity
+
+G, K, M, T, S = 2, 1024, 128, 2048, 512
+FLOPS = 2 * 2 * K * S * M
+
+F32 = mybir.dt.float32
+BF16 = mybir.dt.bfloat16
+I32 = mybir.dt.int32
+U32 = mybir.dt.uint32
+U16 = mybir.dt.uint16
+U8 = mybir.dt.uint8
+FP8X4 = mybir.dt.float8_e4m3fn_x4
+FP4X4 = mybir.dt.float4_e2m1fn_x4
+GELU = mybir.ActivationFunctionType.Gelu_apprx_tanh
+
+P = 128
+PASSES = 2
+HALF = S // 2
+LIST_ROWS = 16
+
+PLAN_BODY = [[("scalar", 1024)], [("vector", 640), ("scalar", 384)]]
+PLAN_THIRD = [[("scalar", 1024)], [("vector", 384), ("scalar", 640)]]
+PLAN_LAST = [[("scalar", 1024)], [("vector", 512)], [("vector", 320), ("scalar", 192)]]
+
+
+def tile_list_sage_tm_gelu_kernel(
+    tc, xT, c, w4_words, w4_scales, w8_words, w8_scales, b, offs, out
+):
+    nc = tc.nc
+    with ExitStack() as ctx:
+        lists = ctx.enter_context(tc.tile_pool(name="lists", bufs=1))
+        keep = ctx.enter_context(tc.tile_pool(name="keep", bufs=1))
+        psum = ctx.enter_context(tc.psum_pool(name="psum", bufs=1))
+
+        offsets = lists.tile([P, G * S // LIST_ROWS], U16, name="offsets")
+        x_rows = xT.rearrange("(a p u e) t -> a u p e t", a=PASSES, p=P, u=2, e=2)
+        c_rows = c.rearrange("(a p i) j -> a p i j", a=PASSES, p=P, i=4)
+
+        staged = {}
+        for a in range(PASSES):
+            for u in range(2):
+                plan = [[PLAN_BODY, PLAN_BODY], [PLAN_THIRD, PLAN_LAST]][a][u]
+                t0 = 0
+                for n, shares in enumerate(plan):
+                    width = sum(cols for eng, cols in shares)
+                    raw = keep.tile([P, 2, width], F32, name="x_raw_%d_%d_%d" % (a, u, n))
+                    nc.sync.dma_start(out=raw[:], in_=x_rows[a, u][:, :, t0 : t0 + width])
+                    staged[(a, u, n)] = (raw, t0, shares)
+                    t0 = t0 + width
+                    if (a, u, n) == (0, 0, 0):
+                        nc.sync.dma_start(offsets[:], offs)
+        c_raw = {}
+        for h in range(2):
+            for a in range(PASSES):
+                raw = keep.tile([P, 4, HALF], F32, name="c_raw_%d_%d" % (a, h))
+                nc.sync.dma_start(out=raw[:], in_=c_rows[a][:, :, h * HALF : (h + 1) * HALF])
+                c_raw[(a, h)] = raw
+
+        w4_codes = keep.tile([P, PASSES, 2 * M], U8, name="w4_codes", align_bytes=64)
+        w8_codes = keep.tile([P, PASSES, 4 * M], U8, name="w8_codes", align_bytes=64)
+        w4_plane = keep.tile([P, PASSES, M], U8, name="w4_plane", align_bytes=64)
+        w8_plane = keep.tile([P, PASSES, M], U8, name="w8_plane", align_bytes=64)
+        b_column = keep.tile([P, 1], F32, name="b_column")
+        nc.scalar.dma_start(out=b_column[:], in_=b.rearrange("(p o) -> p o", o=1))
+        nc.scalar.dma_start(out=w4_codes[:].bitcast(I32), in_=w4_words.rearrange("a p n -> p a n").bitcast(I32))
+        nc.scalar.dma_start(out=w8_codes[:].bitcast(I32), in_=w8_words.rearrange("a p n i -> p a (n i)").bitcast(I32))
+        for plane, scales in ((w4_plane, w4_scales), (w8_plane, w8_scales)):
+            nc.vector.memset(plane[:].bitcast(I32), 0)
+            for q in range(4):
+                nc.gpsimd.dma_start(
+                    out=plane[32 * q : 32 * q + 4].bitcast(I32),
+                    in_=scales[:, 4 * q : 4 * q + 4, :].rearrange("a r n -> r a n").bitcast(I32),
+                )
+
+        warm_in = keep.tile([P, 1], F32, name="warm_in")
+        warm_out = keep.tile([P, 1], F32, name="warm_out")
+        nc.vector.memset(warm_in[:], 0.0)
+        nc.scalar.activation(out=warm_out[:], in_=warm_in[:], func=GELU)
+
+        identity = keep.tile([P, P], F32, name="identity")
+        make_identity(nc, identity[:])
+        b_psum = psum.tile([P, M], F32, name="b_psum")
+        nc.tensor.transpose(b_psum[:], b_column[:, 0:1].to_broadcast([P, P]), identity[:])
+        b_rows = keep.tile([P, 1, M], F32, name="b_rows")
+        nc.vector.tensor_copy(out=b_rows[:, 0, :], in_=b_psum[:])
+
+        def quantise(grouped, width, name):
+            codes = keep.tile([P, width], U32, name=name + "_codes", align_bytes=64)
+            plane = keep.tile([P, width], U8, name=name + "_plane", align_bytes=64)
+            nc.vector.quantize_mx(out=codes[:].bitcast(FP8X4), scales=plane[:], in_=grouped[:])
+            return codes, plane
+
+        def cast_pair(a, u):
+            pair = keep.tile([P, T], U32, name="pair_%d_%d" % (a, u))
+            halves = pair[:].bitcast(BF16).rearrange("p (t e) -> p t e", e=2)
+            n = 0
+            while (a, u, n) in staged:
+                raw, t0, shares = staged[(a, u, n)]
+                s0 = 0
+                for eng, cols in shares:
+                    dst = halves[:, t0 + s0 : t0 + s0 + cols, :]
+                    src = raw[:, :, s0 : s0 + cols].rearrange("p e t -> p t e")
+                    if eng == "scalar":
+                        nc.scalar.copy(out=dst, in_=src)
+                    else:
+                        nc.vector.tensor_copy(out=dst, in_=src)
+                    s0 = s0 + cols
+                n = n + 1
+            return pair
+
+        def gather(pair, picked, u, j0, width):
+            for g in range(G):
+                col = (g * S + j0) // LIST_ROWS
+                nc.vector.tensor_copy(
+                    out=picked[:, u, g, :],
+                    in_=pair[:].indirect(offsets[:, col : col + width // LIST_ROWS]),
+                )
+
+        def maximum(picked, width, name):
+            grouped = keep.tile([P, 4 * width], BF16, name=name, align_bytes=64)
+            sides = [
+                picked[:, :, g, :].bitcast(BF16).rearrange("p u (j e) -> p j u e", e=2) for g in range(G)
+            ]
+            nc.vector.tensor_tensor(
+                out=grouped[:].rearrange("p (j u e) -> p j u e", u=2, e=2),
+                in0=sides[0],
+                in1=sides[1],
+                op=mybir.AluOpType.max,
+            )
+            return grouped
+
+        picked0 = keep.tile([P, 2, G, S], U32, name="picked_0")
+        for u in range(2):
+            gather(cast_pair(0, u), picked0, u, 0, S)
+        xm0 = quantise(maximum(picked0, S, "xm_0"), S, "xm_0")
+
+        picked1 = [keep.tile([P, 2, G, HALF], U32, name="picked_1_%d" % h) for h in range(2)]
+        for u in range(2):
+            pair = cast_pair(1, u)
+            for h in range(2):
+                gather(pair, picked1[h], u, h * HALF, HALF)
+        xm1 = [quantise(maximum(picked1[h], HALF, "xm_1_%d" % h), HALF, "xm_1_%d" % h) for h in range(2)]
+
+        cq = {}
+        for h in range(2):
+            for a in range(PASSES):
+                grouped = keep.tile([P, 4 * HALF], BF16, name="c_%d_%d" % (a, h), tag="c_%d_%d" % (a, h), align_bytes=64)
+                nc.scalar.copy(
+                    out=grouped[:].rearrange("p (m r i) -> p m i r", r=4, i=4),
+                    in_=c_raw[(a, h)][:].rearrange("p i (m r) -> p m i r", r=4),
+                )
+                cq[(a, h)] = quantise(grouped, HALF, "c_%d_%d" % (a, h))
+
+        for h in range(2):
+            acc = psum.tile([P, 2, M], F32, name="acc_%d" % h)
+            operands = [
+                (xm0, h * HALF, w4_codes[:, 0, :].bitcast(FP4X4), w4_plane[:, 0, :]),
+                (xm1[h], 0, w4_codes[:, 1, :].bitcast(FP4X4), w4_plane[:, 1, :]),
+                (cq[(0, h)], 0, w8_codes[:, 0, :].bitcast(FP8X4), w8_plane[:, 0, :]),
+                (cq[(1, h)], 0, w8_codes[:, 1, :].bitcast(FP8X4), w8_plane[:, 1, :]),
+            ]
+            for n, ((codes, plane), j0, w_codes, w_plane) in enumerate(operands):
+                for r in range(2):
+                    cols = slice(j0 + r * P, j0 + (r + 1) * P)
+                    nc.tensor.matmul_mx(
+                        out=acc[:, r, :],
+                        lhsT=codes[:, cols].bitcast(FP8X4),
+                        lhsT_scale=plane[:, cols],
+                        rhs=w_codes,
+                        rhs_scale=w_plane,
+                        start=(n == 0 and r == 0),
+                        stop=(n == len(operands) - 1 and r == 1),
+                    )
+            biased = keep.tile([P, 2, M], F32, name="biased_%d" % h, tag="c_1_%d" % (1 - h), align_bytes=64)
+            nc.vector.tensor_tensor(
+                out=biased[:], in0=acc[:], in1=b_rows[:].to_broadcast([P, 2, M]), op=mybir.AluOpType.add
+            )
+            result = keep.tile([P, 2, M], F32, name="result_%d" % h)
+            nc.scalar.activation(out=result[:], in_=biased[:], func=GELU)
+            nc.sync.dma_start(
+                out=out[h * HALF : (h + 1) * HALF, :].rearrange("(r p) n -> p r n", p=P), in_=result[:]
+            )

@@ -21,9 +21,18 @@ PASSES = 2
 HALF = S // 2
 LIST_ROWS = 16
 
-PLAN_BODY = [[("scalar", 1024)], [("vector", 640), ("scalar", 384)]]
-PLAN_THIRD = [[("scalar", 1024)], [("vector", 384), ("scalar", 640)]]
-PLAN_LAST = [[("scalar", 1024)], [("vector", 512)], [("vector", 320), ("scalar", 192)]]
+C_PIECES = [(0, 0, 256), (1, 0, 256), (0, 256, 256), (1, 256, 128), (1, 384, 128)]
+OUT_GROUPS = [(0, 2), (2, 1), (3, 1)]
+X_PLAN = [
+    [
+        [[("vector", 512), ("scalar", 768)], [("vector", 512), ("scalar", 256)]],
+        [[("vector", 768), ("scalar", 640)], [("vector", 416), ("scalar", 224)]],
+    ],
+    [
+        [[("scalar", 1024)], [("vector", 416), ("scalar", 608)]],
+        [[("scalar", 768)], [("vector", 256), ("scalar", 512)], [("vector", 320), ("scalar", 192)]],
+    ],
+]
 
 
 def tile_list_sage_tm_gelu_kernel(
@@ -42,7 +51,7 @@ def tile_list_sage_tm_gelu_kernel(
         staged = {}
         for a in range(PASSES):
             for u in range(2):
-                plan = [[PLAN_BODY, PLAN_BODY], [PLAN_THIRD, PLAN_LAST]][a][u]
+                plan = X_PLAN[a][u]
                 t0 = 0
                 for n, shares in enumerate(plan):
                     width = sum(cols for eng, cols in shares)
@@ -52,33 +61,33 @@ def tile_list_sage_tm_gelu_kernel(
                     t0 = t0 + width
                     if (a, u, n) == (0, 0, 0):
                         nc.sync.dma_start(offsets[:], offs)
-        c_raw = {}
-        for h in range(2):
-            for a in range(PASSES):
-                raw = keep.tile([P, 4, HALF], F32, name="c_raw_%d_%d" % (a, h))
-                nc.sync.dma_start(out=raw[:], in_=c_rows[a][:, :, h * HALF : (h + 1) * HALF])
-                c_raw[(a, h)] = raw
-
         w4_codes = keep.tile([P, PASSES, 2 * M], U8, name="w4_codes", align_bytes=64)
         w8_codes = keep.tile([P, PASSES, 4 * M], U8, name="w8_codes", align_bytes=64)
         w4_plane = keep.tile([P, PASSES, M], U8, name="w4_plane", align_bytes=64)
         w8_plane = keep.tile([P, PASSES, M], U8, name="w8_plane", align_bytes=64)
-        b_column = keep.tile([P, 1], F32, name="b_column")
-        nc.scalar.dma_start(out=b_column[:], in_=b.rearrange("(p o) -> p o", o=1))
-        nc.scalar.dma_start(out=w4_codes[:].bitcast(I32), in_=w4_words.rearrange("a p n -> p a n").bitcast(I32))
-        nc.scalar.dma_start(out=w8_codes[:].bitcast(I32), in_=w8_words.rearrange("a p n i -> p a (n i)").bitcast(I32))
-        for plane, scales in ((w4_plane, w4_scales), (w8_plane, w8_scales)):
-            nc.vector.memset(plane[:].bitcast(I32), 0)
+        nc.gpsimd.memset(w4_plane[:].bitcast(I32), 0)
+        nc.gpsimd.memset(w8_plane[:].bitcast(I32), 0)
+
+        def load_weight(codes, words, plane, scales):
+            nc.sync.dma_start(out=codes[:].bitcast(I32), in_=words.bitcast(I32))
             for q in range(4):
-                nc.gpsimd.dma_start(
+                nc.sync.dma_start(
                     out=plane[32 * q : 32 * q + 4].bitcast(I32),
                     in_=scales[:, 4 * q : 4 * q + 4, :].rearrange("a r n -> r a n").bitcast(I32),
                 )
 
-        warm_in = keep.tile([P, 1], F32, name="warm_in")
-        warm_out = keep.tile([P, 1], F32, name="warm_out")
-        nc.vector.memset(warm_in[:], 0.0)
-        nc.scalar.activation(out=warm_out[:], in_=warm_in[:], func=GELU)
+        c_raw = []
+        for n, (a, j0, width) in enumerate(C_PIECES):
+            raw = keep.tile([P, 4, width], F32, name="c_raw_%d" % n)
+            nc.sync.dma_start(out=raw[:], in_=c_rows[a][:, :, j0 : j0 + width])
+            c_raw.append(raw)
+            if n == 0:
+                load_weight(w4_codes, w4_words.rearrange("a p n -> p a n"), w4_plane, w4_scales)
+            if n == 2:
+                load_weight(w8_codes, w8_words.rearrange("a p n i -> p a (n i)"), w8_plane, w8_scales)
+
+        b_column = keep.tile([P, 1], F32, name="b_column")
+        nc.scalar.dma_start(out=b_column[:], in_=b.rearrange("(p o) -> p o", o=1))
 
         identity = keep.tile([P, P], F32, name="identity")
         make_identity(nc, identity[:])
@@ -101,8 +110,8 @@ def tile_list_sage_tm_gelu_kernel(
                 raw, t0, shares = staged[(a, u, n)]
                 s0 = 0
                 for eng, cols in shares:
-                    dst = halves[:, t0 + s0 : t0 + s0 + cols, :]
-                    src = raw[:, :, s0 : s0 + cols].rearrange("p e t -> p t e")
+                    dst = halves[:, t0 + s0 : t0 + s0 + cols, :].rearrange("p (m r) e -> p m e r", r=4)
+                    src = raw[:, :, s0 : s0 + cols].rearrange("p e (m r) -> p m e r", r=4)
                     if eng == "scalar":
                         nc.scalar.copy(out=dst, in_=src)
                     else:
@@ -111,75 +120,71 @@ def tile_list_sage_tm_gelu_kernel(
                 n = n + 1
             return pair
 
-        def gather(pair, picked, u, j0, width):
-            for g in range(G):
-                col = (g * S + j0) // LIST_ROWS
-                nc.vector.tensor_copy(
-                    out=picked[:, u, g, :],
-                    in_=pair[:].indirect(offsets[:, col : col + width // LIST_ROWS]),
+        operands = {}
+        for a, width in enumerate((S, HALF)):
+            starts = range(0, S, width)
+            picked = [keep.tile([P, 2, G * width], U32, name="picked_%d_%d" % (a, j0)) for j0 in starts]
+            for u in range(2):
+                pair = cast_pair(a, u)
+                if width == S:
+                    nc.vector.tensor_copy(out=picked[0][:, u, :], in_=pair[:].indirect(offsets[:]))
+                    continue
+                for n, j0 in enumerate(starts):
+                    for g in range(G):
+                        col = (g * S + j0) // LIST_ROWS
+                        nc.vector.tensor_copy(
+                            out=picked[n][:, u, g * width : (g + 1) * width],
+                            in_=pair[:].indirect(offsets[:, col : col + width // LIST_ROWS]),
+                        )
+            for n, j0 in enumerate(starts):
+                grouped = keep.tile([P, 4 * width], BF16, name="xm_%d_%d" % (a, j0), align_bytes=64)
+                sides = [
+                    picked[n][:, :, g * width : (g + 1) * width].bitcast(BF16).rearrange("p u (j e) -> p j u e", e=2)
+                    for g in range(G)
+                ]
+                nc.vector.tensor_tensor(
+                    out=grouped[:].rearrange("p (j u e) -> p j u e", u=2, e=2),
+                    in0=sides[0],
+                    in1=sides[1],
+                    op=mybir.AluOpType.max,
                 )
+                codes, plane = quantise(grouped, width, "xm_%d_%d" % (a, j0))
+                for r in range(width // P):
+                    operands[("xm", a, j0 // P + r)] = (codes, plane, r * P)
 
-        def maximum(picked, width, name):
-            grouped = keep.tile([P, 4 * width], BF16, name=name, align_bytes=64)
-            sides = [
-                picked[:, :, g, :].bitcast(BF16).rearrange("p u (j e) -> p j u e", e=2) for g in range(G)
-            ]
-            nc.vector.tensor_tensor(
-                out=grouped[:].rearrange("p (j u e) -> p j u e", u=2, e=2),
-                in0=sides[0],
-                in1=sides[1],
-                op=mybir.AluOpType.max,
+        for n, (a, j0, width) in enumerate(C_PIECES):
+            grouped = keep.tile([P, 4 * width], BF16, name="c_%d" % n, tag="c_%d" % n, align_bytes=64)
+            nc.scalar.copy(
+                out=grouped[:].rearrange("p (m r i) -> p m i r", r=4, i=4),
+                in_=c_raw[n][:].rearrange("p i (m r) -> p m i r", r=4),
             )
-            return grouped
+            codes, plane = quantise(grouped, width, "c_%d" % n)
+            for r in range(width // P):
+                operands[("c", a, j0 // P + r)] = (codes, plane, r * P)
 
-        picked0 = keep.tile([P, 2, G, S], U32, name="picked_0")
-        for u in range(2):
-            gather(cast_pair(0, u), picked0, u, 0, S)
-        xm0 = quantise(maximum(picked0, S, "xm_0"), S, "xm_0")
-
-        picked1 = [keep.tile([P, 2, G, HALF], U32, name="picked_1_%d" % h) for h in range(2)]
-        for u in range(2):
-            pair = cast_pair(1, u)
-            for h in range(2):
-                gather(pair, picked1[h], u, h * HALF, HALF)
-        xm1 = [quantise(maximum(picked1[h], HALF, "xm_1_%d" % h), HALF, "xm_1_%d" % h) for h in range(2)]
-
-        cq = {}
-        for h in range(2):
-            for a in range(PASSES):
-                grouped = keep.tile([P, 4 * HALF], BF16, name="c_%d_%d" % (a, h), tag="c_%d_%d" % (a, h), align_bytes=64)
-                nc.scalar.copy(
-                    out=grouped[:].rearrange("p (m r i) -> p m i r", r=4, i=4),
-                    in_=c_raw[(a, h)][:].rearrange("p i (m r) -> p m i r", r=4),
-                )
-                cq[(a, h)] = quantise(grouped, HALF, "c_%d_%d" % (a, h))
-
-        for h in range(2):
-            acc = psum.tile([P, 2, M], F32, name="acc_%d" % h)
-            operands = [
-                (xm0, h * HALF, w4_codes[:, 0, :].bitcast(FP4X4), w4_plane[:, 0, :]),
-                (xm1[h], 0, w4_codes[:, 1, :].bitcast(FP4X4), w4_plane[:, 1, :]),
-                (cq[(0, h)], 0, w8_codes[:, 0, :].bitcast(FP8X4), w8_plane[:, 0, :]),
-                (cq[(1, h)], 0, w8_codes[:, 1, :].bitcast(FP8X4), w8_plane[:, 1, :]),
-            ]
-            for n, ((codes, plane), j0, w_codes, w_plane) in enumerate(operands):
-                for r in range(2):
-                    cols = slice(j0 + r * P, j0 + (r + 1) * P)
+        weights = [("xm", a, w4_codes[:, a, :].bitcast(FP4X4), w4_plane[:, a, :]) for a in range(PASSES)]
+        weights = weights + [("c", a, w8_codes[:, a, :].bitcast(FP8X4), w8_plane[:, a, :]) for a in range(PASSES)]
+        biased_all = keep.tile([P, S // P, M], F32, name="biased", tag="c_%d" % (len(C_PIECES) - 1), align_bytes=64)
+        for tile0, tiles in OUT_GROUPS:
+            biased = biased_all[:, tile0 : tile0 + tiles, :]
+            acc = psum.tile([P, tiles, M], F32, name="acc_%d" % tile0)
+            for n, (kind, a, w_codes, w_plane) in enumerate(weights):
+                for r in range(tiles):
+                    codes, plane, j0 = operands[(kind, a, tile0 + r)]
                     nc.tensor.matmul_mx(
                         out=acc[:, r, :],
-                        lhsT=codes[:, cols].bitcast(FP8X4),
-                        lhsT_scale=plane[:, cols],
+                        lhsT=codes[:, j0 : j0 + P].bitcast(FP8X4),
+                        lhsT_scale=plane[:, j0 : j0 + P],
                         rhs=w_codes,
                         rhs_scale=w_plane,
                         start=(n == 0 and r == 0),
-                        stop=(n == len(operands) - 1 and r == 1),
+                        stop=(n == len(weights) - 1 and r == tiles - 1),
                     )
-            biased = keep.tile([P, 2, M], F32, name="biased_%d" % h, tag="c_1_%d" % (1 - h), align_bytes=64)
             nc.vector.tensor_tensor(
-                out=biased[:], in0=acc[:], in1=b_rows[:].to_broadcast([P, 2, M]), op=mybir.AluOpType.add
+                out=biased, in0=acc[:], in1=b_rows[:].to_broadcast([P, tiles, M]), op=mybir.AluOpType.add
             )
-            result = keep.tile([P, 2, M], F32, name="result_%d" % h)
-            nc.scalar.activation(out=result[:], in_=biased[:], func=GELU)
+            result = keep.tile([P, tiles, M], F32, name="result_%d" % tile0)
+            nc.scalar.activation(out=result[:], in_=biased, func=GELU)
             nc.sync.dma_start(
-                out=out[h * HALF : (h + 1) * HALF, :].rearrange("(r p) n -> p r n", p=P), in_=result[:]
+                out=out[tile0 * P : (tile0 + tiles) * P, :].rearrange("(r p) n -> p r n", p=P), in_=result[:]
             )

@@ -23,6 +23,7 @@ LIST_ROWS = 16
 
 C_PIECES = [(0, 0, 256), (1, 0, 256), (0, 256, 256), (1, 256, 128), (1, 384, 128)]
 OUT_GROUPS = [(0, 2), (2, 1), (3, 1)]
+C_LAST_ON_VECTOR = 80
 X_PLAN = [
     [
         [[("vector", 512), ("scalar", 768)], [("vector", 512), ("scalar", 256)]],
@@ -89,6 +90,11 @@ def tile_list_sage_tm_gelu_kernel(
         b_column = keep.tile([P, 1], F32, name="b_column")
         nc.scalar.dma_start(out=b_column[:], in_=b.rearrange("(p o) -> p o", o=1))
 
+        warm_in = keep.tile([P, 1], F32, name="warm_in")
+        warm_out = keep.tile([P, 1], F32, name="warm_out")
+        nc.vector.memset(warm_in[:], 0.0)
+        nc.scalar.activation(out=warm_out[:], in_=warm_in[:], func=GELU)
+
         identity = keep.tile([P, P], F32, name="identity")
         make_identity(nc, identity[:])
         b_psum = psum.tile([P, M], F32, name="b_psum")
@@ -154,10 +160,16 @@ def tile_list_sage_tm_gelu_kernel(
 
         for n, (a, j0, width) in enumerate(C_PIECES):
             grouped = keep.tile([P, 4 * width], BF16, name="c_%d" % n, tag="c_%d" % n, align_bytes=64)
+            on_vector = C_LAST_ON_VECTOR if n == len(C_PIECES) - 1 else 0
             nc.scalar.copy(
-                out=grouped[:].rearrange("p (m r i) -> p m i r", r=4, i=4),
-                in_=c_raw[n][:].rearrange("p i (m r) -> p m i r", r=4),
+                out=grouped[:, 4 * on_vector :].rearrange("p (m r i) -> p m i r", r=4, i=4),
+                in_=c_raw[n][:, :, on_vector:].rearrange("p i (m r) -> p m i r", r=4),
             )
+            if on_vector:
+                nc.vector.tensor_copy(
+                    out=grouped[:, : 4 * on_vector].rearrange("p (m r i) -> p m i r", r=4, i=4),
+                    in_=c_raw[n][:, :, :on_vector].rearrange("p i (m r) -> p m i r", r=4),
+                )
             codes, plane = quantise(grouped, width, "c_%d" % n)
             for r in range(width // P):
                 operands[("c", a, j0 // P + r)] = (codes, plane, r * P)

@@ -63,7 +63,7 @@ def tile_list_sage_tm_gelu_kernel(
                     if (a, u, n) == (0, 0, 0):
                         nc.sync.dma_start(offsets[:], offs)
         w4_codes = keep.tile([P, PASSES, 2 * M], U8, name="w4_codes", align_bytes=64)
-        w8_codes = keep.tile([P, PASSES, 4 * M], U8, name="w8_codes", align_bytes=64)
+        w8_codes = [keep.tile([P, 4 * M], U8, name="w8_codes_%d" % a, align_bytes=64) for a in range(PASSES)]
         w4_plane = keep.tile([P, PASSES, M], U8, name="w4_plane", align_bytes=64)
         w8_plane = keep.tile([P, PASSES, M], U8, name="w8_plane", align_bytes=64)
         nc.gpsimd.memset(w4_plane[:].bitcast(I32), 0)
@@ -85,7 +85,8 @@ def tile_list_sage_tm_gelu_kernel(
             if n == 0:
                 load_weight(w4_codes, w4_words.rearrange("a p n -> p a n"), w4_plane, w4_scales)
             if n == 2:
-                load_weight(w8_codes, w8_words.rearrange("a p n i -> p a (n i)"), w8_plane, w8_scales)
+                load_weight(w8_codes[0], w8_words[0].rearrange("p n i -> p (n i)"), w8_plane, w8_scales)
+        nc.sync.dma_start(out=w8_codes[1][:].bitcast(I32), in_=w8_words[1].rearrange("p n i -> p (n i)").bitcast(I32))
 
         b_column = keep.tile([P, 1], F32, name="b_column")
         nc.scalar.dma_start(out=b_column[:], in_=b.rearrange("(p o) -> p o", o=1))
@@ -175,7 +176,7 @@ def tile_list_sage_tm_gelu_kernel(
                 operands[("c", a, j0 // P + r)] = (codes, plane, r * P)
 
         weights = [("xm", a, w4_codes[:, a, :].bitcast(FP4X4), w4_plane[:, a, :]) for a in range(PASSES)]
-        weights = weights + [("c", a, w8_codes[:, a, :].bitcast(FP8X4), w8_plane[:, a, :]) for a in range(PASSES)]
+        weights = weights + [("c", a, w8_codes[a][:].bitcast(FP8X4), w8_plane[:, a, :]) for a in range(PASSES)]
         biased_all = keep.tile([P, S // P, M], F32, name="biased", tag="c_%d" % (len(C_PIECES) - 1), align_bytes=64)
         for tile0, tiles in OUT_GROUPS:
             biased = biased_all[:, tile0 : tile0 + tiles, :]

from contextlib import ExitStack

import concourse.mybir as mybir
from concourse.masks import make_identity

G, K, M, T, S = 2, 1024, 128, 2048, 512
FLOPS = 2 * 2 * K * S * M

F32 = mybir.dt.float32
BF16 = mybir.dt.bfloat16
I32 = mybir.dt.int32
U32 = mybir.dt.uint32
U16 = mybir.dt.uint16
U8 = mybir.dt.uint8
FP8X4 = mybir.dt.float8_e4m3fn_x4
FP4X4 = mybir.dt.float4_e2m1fn_x4
GELU = mybir.ActivationFunctionType.Gelu_apprx_tanh

P = 128
PASSES = 2
HALF = S // 2
LIST_ROWS = 16

C_PIECES = [(0, 0, 256), (1, 0, 256), (0, 256, 256), (1, 256, 128), (1, 384, 128)]
OUT_GROUPS = [(0, 2), (2, 1), (3, 1)]
C_LAST_ON_VECTOR = 80
X_PLAN = [
    [
        [[("vector", 512), ("scalar", 768)], [("vector", 512), ("scalar", 256)]],
        [[("vector", 768), ("scalar", 640)], [("vector", 416), ("scalar", 224)]],
    ],
    [
        [[("scalar", 1024)], [("vector", 416), ("scalar", 608)]],
        [[("scalar", 768)], [("vector", 256), ("scalar", 512)], [("vector", 320), ("scalar", 192)]],
    ],
]


def tile_list_sage_tm_gelu_kernel(
    tc, xT, c, w4_words, w4_scales, w8_words, w8_scales, b, offs, out
):
    nc = tc.nc
    with ExitStack() as ctx:
        lists = ctx.enter_context(tc.tile_pool(name="lists", bufs=1))
        keep = ctx.enter_context(tc.tile_pool(name="keep", bufs=1))
        psum = ctx.enter_context(tc.psum_pool(name="psum", bufs=1))

        offsets = lists.tile([P, G * S // LIST_ROWS], U16, name="offsets")
        x_rows = xT.rearrange("(a p u e) t -> a u p e t", a=PASSES, p=P, u=2, e=2)
        c_rows = c.rearrange("(a p i) j -> a p i j", a=PASSES, p=P, i=4)

        staged = {}
        for a in range(PASSES):
            for u in range(2):
                plan = X_PLAN[a][u]
                t0 = 0
                for n, shares in enumerate(plan):
                    width = sum(cols for eng, cols in shares)
                    raw = keep.tile([P, 2, width], F32, name="x_raw_%d_%d_%d" % (a, u, n))
                    nc.sync.dma_start(out=raw[:], in_=x_rows[a, u][:, :, t0 : t0 + width])
                    staged[(a, u, n)] = (raw, t0, shares)
                    t0 = t0 + width
                    if (a, u, n) == (0, 0, 0):
                        nc.sync.dma_start(offsets[:], offs)
        w4_codes = keep.tile([P, PASSES, 2 * M], U8, name="w4_codes", align_bytes=64)
        w8_codes = [keep.tile([P, 4 * M], U8, name="w8_codes_%d" % a, align_bytes=64) for a in range(PASSES)]
        w4_plane = keep.tile([P, PASSES, M], U8, name="w4_plane", align_bytes=64)
        w8_plane = keep.tile([P, PASSES, M], U8, name="w8_plane", align_bytes=64)
        nc.gpsimd.memset(w4_plane[:].bitcast(I32), 0)
        nc.gpsimd.memset(w8_plane[:].bitcast(I32), 0)

        def load_weight(codes, words, plane, scales):
            nc.sync.dma_start(out=codes[:].bitcast(I32), in_=words.bitcast(I32))
            for q in range(4):
                nc.sync.dma_start(
                    out=plane[32 * q : 32 * q + 4].bitcast(I32),
                    in_=scales[:, 4 * q : 4 * q + 4, :].rearrange("a r n -> r a n").bitcast(I32),
                )

        c_raw = []
        for n, (a, j0, width) in enumerate(C_PIECES):
            raw = keep.tile([P, 4, width], F32, name="c_raw_%d" % n)
            nc.sync.dma_start(out=raw[:], in_=c_rows[a][:, :, j0 : j0 + width])
            c_raw.append(raw)
            if n == 0:
                load_weight(w4_codes, w4_words.rearrange("a p n -> p a n"), w4_plane, w4_scales)
            if n == 2:
                load_weight(w8_codes[0], w8_words[0].rearrange("p n i -> p (n i)"), w8_plane, w8_scales)
        nc.sync.dma_start(out=w8_codes[1][:].bitcast(I32), in_=w8_words[1].rearrange("p n i -> p (n i)").bitcast(I32))

        b_column = keep.tile([P, 1], F32, name="b_column")
        nc.scalar.dma_start(out=b_column[:], in_=b.rearrange("(p o) -> p o", o=1))

        warm_in = keep.tile([P, 1], F32, name="warm_in")
        warm_out = keep.tile([P, 1], F32, name="warm_out")
        nc.vector.memset(warm_in[:], 0.0)
        nc.scalar.activation(out=warm_out[:], in_=warm_in[:], func=GELU)

        identity = keep.tile([P, P], F32, name="identity")
        make_identity(nc, identity[:])
        b_psum = psum.tile([P, M], F32, name="b_psum")
        nc.tensor.transpose(b_psum[:], b_column[:, 0:1].to_broadcast([P, P]), identity[:])
        b_rows = keep.tile([P, 1, M], F32, name="b_rows")
        nc.vector.tensor_copy(out=b_rows[:, 0, :], in_=b_psum[:])

        def quantise(grouped, width, name):
            codes = keep.tile([P, width], U32, name=name + "_codes", align_bytes=64)
            plane = keep.tile([P, width], U8, name=name + "_plane", align_bytes=64)
            nc.vector.quantize_mx(out=codes[:].bitcast(FP8X4), scales=plane[:], in_=grouped[:])
            return codes, plane

        def cast_pair(a, u):
            pair = keep.tile([P, T], U32, name="pair_%d_%d" % (a, u))
            halves = pair[:].bitcast(BF16).rearrange("p (t e) -> p t e", e=2)
            n = 0
            while (a, u, n) in staged:
                raw, t0, shares = staged[(a, u, n)]
                s0 = 0
                for eng, cols in shares:
                    dst = halves[:, t0 + s0 : t0 + s0 + cols, :].rearrange("p (m r) e -> p m e r", r=4)
                    src = raw[:, :, s0 : s0 + cols].rearrange("p e (m r) -> p m e r", r=4)
                    if eng == "scalar":
                        nc.scalar.copy(out=dst, in_=src)
                    else:
                        nc.vector.tensor_copy(out=dst, in_=src)
                    s0 = s0 + cols
                n = n + 1
            return pair

        operands = {}
        for a, width in enumerate((S, HALF)):
            starts = range(0, S, width)
            picked = [keep.tile([P, 2, G * width], U32, name="picked_%d_%d" % (a, j0)) for j0 in starts]
            for u in range(2):
                pair = cast_pair(a, u)
                if width == S:
                    nc.vector.tensor_copy(out=picked[0][:, u, :], in_=pair[:].indirect(offsets[:]))
                    continue
                for n, j0 in enumerate(starts):
                    for g in range(G):
                        col = (g * S + j0) // LIST_ROWS
                        nc.vector.tensor_copy(
                            out=picked[n][:, u, g * width : (g + 1) * width],
                            in_=pair[:].indirect(offsets[:, col : col + width // LIST_ROWS]),
                        )
            for n, j0 in enumerate(starts):
                grouped = keep.tile([P, 4 * width], BF16, name="xm_%d_%d" % (a, j0), align_bytes=64)
                sides = [
                    picked[n][:, :, g * width : (g + 1) * width].bitcast(BF16).rearrange("p u (j e) -> p j u e", e=2)
                    for g in range(G)
                ]
                nc.vector.tensor_tensor(
                    out=grouped[:].rearrange("p (j u e) -> p j u e", u=2, e=2),
                    in0=sides[0],
                    in1=sides[1],
                    op=mybir.AluOpType.max,
                )
                codes, plane = quantise(grouped, width, "xm_%d_%d" % (a, j0))
                for r in range(width // P):
                    operands[("xm", a, j0 // P + r)] = (codes, plane, r * P)

        for n, (a, j0, width) in enumerate(C_PIECES):
            grouped = keep.tile([P, 4 * width], BF16, name="c_%d" % n, tag="c_%d" % n, align_bytes=64)
            on_vector = C_LAST_ON_VECTOR if n == len(C_PIECES) - 1 else 0
            nc.scalar.copy(
                out=grouped[:, 4 * on_vector :].rearrange("p (m r i) -> p m i r", r=4, i=4),
                in_=c_raw[n][:, :, on_vector:].rearrange("p i (m r) -> p m i r", r=4),
            )
            if on_vector:
                nc.vector.tensor_copy(
                    out=grouped[:, : 4 * on_vector].rearrange("p (m r i) -> p m i r", r=4, i=4),
                    in_=c_raw[n][:, :, :on_vector].rearrange("p i (m r) -> p m i r", r=4),
                )
            codes, plane = quantise(grouped, width, "c_%d" % n)
            for r in range(width // P):
                operands[("c", a, j0 // P + r)] = (codes, plane, r * P)

        weights = [("xm", a, w4_codes[:, a, :].bitcast(FP4X4), w4_plane[:, a, :]) for a in range(PASSES)]
        weights = weights + [("c", a, w8_codes[a][:].bitcast(FP8X4), w8_plane[:, a, :]) for a in range(PASSES)]
        biased_all = keep.tile([P, S // P, M], F32, name="biased", tag="c_%d" % (len(C_PIECES) - 1), align_bytes=64)
        for tile0, tiles in OUT_GROUPS:
            biased = biased_all[:, tile0 : tile0 + tiles, :]
            acc = psum.tile([P, tiles, M], F32, name="acc_%d" % tile0)
            for n, (kind, a, w_codes, w_plane) in enumerate(weights):
                for r in range(tiles):
                    codes, plane, j0 = operands[(kind, a, tile0 + r)]
                    nc.tensor.matmul_mx(
                        out=acc[:, r, :],
                        lhsT=codes[:, j0 : j0 + P].bitcast(FP8X4),
                        lhsT_scale=plane[:, j0 : j0 + P],
                        rhs=w_codes,
                        rhs_scale=w_plane,
                        start=(n == 0 and r == 0),
                        stop=(n == len(weights) - 1 and r == tiles - 1),
                    )
            nc.vector.tensor_tensor(
                out=biased, in0=acc[:], in1=b_rows[:].to_broadcast([P, tiles, M]), op=mybir.AluOpType.add
            )
            result = keep.tile([P, tiles, M], F32, name="result_%d" % tile0)
            nc.scalar.activation(out=result[:], in_=biased, func=GELU)
            nc.sync.dma_start(
                out=out[tile0 * P : (tile0 + tiles) * P, :].rearrange("(r p) n -> p r n", p=P), in_=result[:]
            )
